import numpy as np
import ml_dtypes


def mxq(x, axis, fmt="e4m3"):
    dtype, down = {"e4m3": (ml_dtypes.float8_e4m3fn, 7), "e5m2": (ml_dtypes.float8_e5m2, 14)}[fmt]
    v = np.moveaxis(np.asarray(x, np.float32).astype(ml_dtypes.bfloat16).astype(np.float64), axis, -1)
    blocks = v.reshape(v.shape[:-1] + (-1, 32))
    amax = np.abs(blocks).max(-1, keepdims=True)
    byte = np.maximum(np.where(amax > 0, np.frexp(amax)[1] - 1 + 127, 0) - down, 1)
    scale = np.exp2(byte - 127.0)
    codes = (blocks / scale).astype(np.float32).astype(dtype).astype(np.float64)
    return np.moveaxis((codes * scale).reshape(v.shape), -1, axis)


WIDE = False


def mx_kscale(k):
    if not WIDE:
        return np.ones(k)
    levels = np.array([10, -10, 5, -5, 0])
    if k % 512:
        return np.exp2(np.random.permutation(np.resize(levels, k // 32))).repeat(32)
    a = np.empty((k // 512, 16))
    for p in range(k // 512):
        a[p, :8] = np.random.permutation(np.resize(levels, 8))
        for g in range(8):
            far = levels[np.abs(levels - a[p, g]) >= 10]
            a[p, g + 8] = far[np.random.randint(len(far))]
    return np.exp2(a.ravel()).repeat(32)


BF16 = ml_dtypes.bfloat16


def bf(x):
    return np.asarray(x, np.float32).astype(BF16)


def f64(x):
    return np.asarray(x).astype(np.float64)


E2M1 = np.array([0.0, 0.5, 1.0, 1.5, 2.0, 3.0, 4.0, 6.0, -0.0, -0.5, -1.0, -1.5, -2.0, -3.0, -4.0, -6.0])


def pack_weight(w, fmt):
    k, n = w.shape
    w = f64(bf(w)).reshape(k // 32, 32, n)
    amax = np.abs(w).max(1)
    if fmt == "e4m3":
        byte = np.frexp(amax)[1] - 1 + 127 - 7
    else:
        mant, ex = np.frexp(amax / 6.0)
        byte = np.where(mant > 0.5, ex, ex - 1) + 127
    byte = np.clip(np.where(amax > 0, byte, 1), 1, 254)
    scaled = (w * np.exp2(127.0 - byte)[:, None, :]).reshape(k, n).astype(np.float32)
    by_word = np.ascontiguousarray(scaled.reshape(k // 512, 128, 4, n).transpose(0, 1, 3, 2))
    if fmt == "e4m3":
        words = by_word.astype(ml_dtypes.float8_e4m3fn).view(np.uint8)
    else:
        c = by_word.astype(ml_dtypes.float4_e2m1fn).view(np.uint8) & 0xF
        words = c[..., 0::2] | (c[..., 1::2] << 4)
    return np.ascontiguousarray(words), np.ascontiguousarray(byte.astype(np.uint8).reshape(k // 512, 16, n))


def unpack_weight(words, scales, fmt):
    g, p, n, _ = words.shape
    if fmt == "e4m3":
        vals = np.ascontiguousarray(words).view(ml_dtypes.float8_e4m3fn).astype(np.float64)
    else:
        nib = np.empty((g, p, n, 4), np.uint8)
        nib[..., 0::2] = words & 0xF
        nib[..., 1::2] = words >> 4
        vals = E2M1[nib]
    vals = vals * np.repeat(np.exp2(scales.astype(np.float64) - 127.0), 8, axis=1)[..., None]
    return vals.transpose(0, 1, 3, 2).reshape(g * 512, n)
def pack4(w):
    words, scales = pack_weight(w, "e2m1")
    return words.reshape(words.shape[0], 128, -1), scales


def unpack4(words, scales):
    return unpack_weight(words.reshape(words.shape[0], 128, -1, 2), scales, "e2m1")


M, K, L, R = 1024, 1024, 2048, 1024


def setup_inputs():
    s, t = mx_kscale(K), mx_kscale(L)
    x = (np.arange(M) + np.random.random(M)) / M
    y = (np.arange(L) + np.random.random(L)) / L
    a = np.sqrt(2 / K) * np.cos(np.pi * np.arange(K)[:, None] * x)
    c = np.sqrt(2 / L) * np.cos(np.pi * y[:, None] * np.arange(R))
    v = np.random.standard_normal((K, L))
    a_words, a_scales = pack4(a * s[:, None])
    v_words, v_scales = pack4(v / s[:, None])
    c_words, c_scales = pack_weight(c / t[:, None], "e4m3")
    stiff = (2 * np.arange(R) / R) ** 2 * np.exp(0.1 * np.random.standard_normal(R))
    return {"a_words": a_words, "a_scales": a_scales,
            "v_words": v_words, "v_scales": v_scales,
            "mob": bf(0.25 * (1 + 0.1 * np.random.standard_normal(L)) * t),
            "c_words": c_words, "c_scales": c_scales,
            "lin": bf(np.random.standard_normal((M, R))),
            "damp": bf(1 / (1 + stiff))}


def reference(a_words, a_scales, v_words, v_scales, mob, c_words, c_scales, lin, damp):
    a = unpack4(a_words, a_scales)
    v = unpack4(v_words, v_scales)
    c = unpack_weight(c_words, c_scales, "e4m3")
    u = a.T @ v
    h = u * u * u * f64(mob)
    z = mxq(h, 1, "e4m3") @ c
    return (f64(lin) - z) * f64(damp)

@@ -1,0 +1,271 @@
+from contextlib import ExitStack
+
+import concourse.mybir as mybir
+
+FLOPS = 2 * 1024 * 1024 * 2048 * 2
+
+F32 = mybir.dt.float32
+BF16 = mybir.dt.bfloat16
+I32 = mybir.dt.int32
+U32 = mybir.dt.uint32
+U8 = mybir.dt.uint8
+FP4X4 = mybir.dt.float4_e2m1fn_x4
+FP8X4 = mybir.dt.float8_e4m3fn_x4
+MULT = mybir.AluOpType.mult
+SUB = mybir.AluOpType.subtract
+SQUARE = mybir.ActivationFunctionType.Square
+
+P = 128
+K, M, L, R = 1024, 1024, 2048, 1024
+PACK = 4
+KG = 2
+JG = 4
+CH = 256
+NCH = M // CH
+NI = CH // P
+NL = 512
+STEPS = NCH * JG
+LAST = STEPS - 1
+
+
+def tile_phase_field_step_s4_kernel(
+    tc, a_words, a_scales, v_words, v_scales, mob, c_words, c_scales, lin, damp, out
+):
+    nc = tc.nc
+    with ExitStack() as ctx:
+        keep = ctx.enter_context(tc.tile_pool(name="keep", bufs=1))
+        work = ctx.enter_context(tc.tile_pool(name="work", bufs=4))
+        psum = ctx.enter_context(tc.psum_pool(name="psum", bufs=2))
+
+        vraw = keep.tile([P, KG, 2 * L], U8, name="vraw", align_bytes=64)
+        vsraw = keep.tile([P, KG, L], U8, name="vsraw", align_bytes=64)
+        vw = [keep.tile([P, KG, PACK, P, 2], U8, name=f"vw{j}", align_bytes=64) for j in range(JG)]
+        vs = [keep.tile([P, KG, PACK, P], U8, name=f"vs{j}", align_bytes=64) for j in range(JG)]
+        aw = keep.tile([P, KG, 2 * M], U8, name="aw", align_bytes=64)
+        asc = keep.tile([P, KG, M], U8, name="asc", align_bytes=64)
+        cw = keep.tile([P, JG, R], U32, name="cw", align_bytes=64)
+        csc = keep.tile([P, R], U8, name="csc", align_bytes=64)
+        mobt = keep.tile([P, JG, PACK], BF16, name="mobt")
+        lint = keep.tile([P, M // P, R], BF16, name="lint")
+        dampt = keep.tile([P, R], BF16, name="dampt")
+        dummy = keep.tile([P, 2], F32, name="dummy")
+        hq = [keep.tile([P, CH], U32, name=f"hq{n}", align_bytes=64) for n in range(STEPS)]
+        hs = [keep.tile([P, CH], U8, name=f"hs{n}", align_bytes=64) for n in range(STEPS)]
+
+        ctx.enter_context(tc.manual_schedule())
+
+        nc.vector.memset(vsraw[:].rearrange("p g n -> p (g n)").bitcast(I32), 0)
+        nc.gpsimd.memset(asc[:].rearrange("p g n -> p (g n)").bitcast(I32), 0)
+        nc.vector.memset(dummy[:], 0.0)
+        nc.vector.memset(csc[:].bitcast(I32), 0)
+
+        def load_v_scales():
+            for q in range(4):
+                nc.sync.dma_start(
+                    out=vsraw[32 * q : 32 * q + 4, :, :].bitcast(I32),
+                    in_=v_scales[:, 4 * q : 4 * q + 4, :].rearrange("g r n -> r g n").bitcast(I32),
+                )
+
+        def load_v_words(lo, hi):
+            cols = slice(2 * lo, 2 * hi)
+            nc.sync.dma_start(
+                out=vraw[:, :, cols].bitcast(I32),
+                in_=v_words.rearrange("g p b -> p g b")[:, :, cols].bitcast(I32),
+            )
+
+        def load_a_words(lo, hi):
+            cols = slice(2 * lo, 2 * hi)
+            nc.sync.dma_start(
+                out=aw[:, :, cols].bitcast(I32),
+                in_=a_words.rearrange("g p b -> p g b")[:, :, cols].bitcast(I32),
+            )
+
+        def load_c_words(g):
+            nc.sync.dma_start(
+                out=cw[:, g, :].bitcast(I32),
+                in_=c_words[g].rearrange("p n t -> p (n t)").bitcast(I32),
+            )
+
+        def load_lin(i):
+            nc.sync.dma_start(out=lint[:, i, :], in_=lin[P * i : P * (i + 1), :])
+
+        load_v_words(0, 1024)
+        load_v_scales()
+        load_a_words(0, CH)
+        for q in range(4):
+            engine = nc.scalar if q < 2 else nc.gpsimd
+            engine.dma_start(
+                out=asc[32 * q : 32 * q + 4, :, :].bitcast(I32),
+                in_=a_scales[:, 4 * q : 4 * q + 4, :].rearrange("g r n -> r g n").bitcast(I32),
+            )
+        nc.scalar.activation(dummy[:, 1:2], dummy[:, 0:1], SQUARE)
+        nc.gpsimd.dma_start(out=mobt[:], in_=mob.rearrange("(j p t) -> p j t", p=P, t=PACK))
+        load_v_words(1024, L)
+        load_a_words(CH, M)
+        load_c_words(0)
+        for q in range(4):
+            nc.sync.dma_start(
+                out=csc[32 * q : 32 * q + 16, :].bitcast(I32),
+                in_=c_scales[:, 4 * q : 4 * q + 4, :].bitcast(I32),
+            )
+        load_c_words(1)
+        load_c_words(2)
+        load_c_words(3)
+        load_lin(0)
+        load_lin(1)
+        nc.sync.dma_start(out=dampt[:], in_=damp.partition_broadcast(P))
+        for i in range(2, M // P):
+            load_lin(i)
+
+        u = {}
+        sq = {}
+        ht = {}
+        hi = {}
+        z = {}
+        res = {}
+
+        def permute_v(j):
+            for g in range(KG):
+                cols = slice(1024 * j, 1024 * (j + 1))
+                nc.vector.tensor_copy(
+                    out=vw[j][:, g],
+                    in_=vraw[:, g, cols].rearrange("p (m t b) -> p t m b", t=PACK, b=2),
+                )
+            nc.vector.tensor_copy(
+                out=vs[j][:],
+                in_=vsraw[:, :, 512 * j : 512 * (j + 1)].rearrange("p g (m t) -> p g t m", t=PACK),
+            )
+
+        def field(n):
+            c, j = divmod(n, JG)
+            for h in range(2):
+                bank = psum.tile([P, 2, CH], F32, tag=f"u{h}", bufs=2, name=f"u{n}_{h}")
+                u[n, h] = bank
+                for e in range(2):
+                    t = 2 * h + e
+                    for g in range(KG):
+                        nc.tensor.matmul_mx(
+                            out=bank[:, e, :],
+                            lhsT=vw[j][:, g, t].rearrange("p m b -> p (m b)").bitcast(FP4X4),
+                            lhsT_scale=vs[j][:, g, t],
+                            rhs=aw[:, g, 2 * CH * c : 2 * CH * (c + 1)].bitcast(FP4X4),
+                            rhs_scale=asc[:, g, CH * c : CH * (c + 1)],
+                            start=(g == 0),
+                            stop=(g == KG - 1),
+                        )
+
+        def square(n, h):
+            sq[n, h] = work.tile([P, 2, CH], F32, tag="sq", name=f"sq{n}_{h}")
+            nc.scalar.activation(sq[n, h][:], u[n, h][:], SQUARE)
+
+        def cube(n, h):
+            j = n % JG
+            if h == 0:
+                ht[n] = work.tile([P, PACK, CH], BF16, tag="ht", name=f"ht{n}", align_bytes=64)
+            for e in range(2):
+                t = 2 * h + e
+                nc.vector.scalar_tensor_tensor(
+                    out=ht[n][:, t, :],
+                    in0=u[n, h][:, e, :],
+                    scalar=mobt[:, j, t : t + 1],
+                    in1=sq[n, h][:, e, :],
+                    op0=MULT,
+                    op1=MULT,
+                )
+
+        def interleave(n):
+            hi[n] = work.tile([P, CH, PACK], BF16, tag="hi", name=f"hi{n}", align_bytes=64)
+            nc.scalar.copy(
+                hi[n][:].rearrange("p (c i) t -> p c t i", i=4),
+                ht[n][:].rearrange("p t (c i) -> p c t i", i=4),
+            )
+
+        def quantise(n):
+            nc.vector.quantize_mx(
+                out=hq[n][:].bitcast(FP8X4),
+                scales=hs[n][:],
+                in_=hi[n][:].rearrange("p n t -> p (n t)"),
+            )
+
+        def analyse(n, b):
+            c, j = divmod(n, JG)
+            i, l = divmod(b, 2)
+            if j == 0:
+                z[c, b] = psum.tile([P, NL], F32, tag=f"z{b}", bufs=1, name=f"z{c}_{b}")
+            nc.tensor.matmul_mx(
+                out=z[c, b][:],
+                lhsT=hq[n][:, P * i : P * (i + 1)].bitcast(FP8X4),
+                lhsT_scale=hs[n][:, P * i : P * (i + 1)],
+                rhs=cw[:, j, NL * l : NL * (l + 1)].bitcast(FP8X4),
+                rhs_scale=csc[4 * j : P, NL * l : NL * (l + 1)],
+                start=(j == 0),
+                stop=(j == JG - 1),
+            )
+
+        def subtract(c, b):
+            i, l = divmod(b, 2)
+            cols = slice(NL * l, NL * (l + 1))
+            res[c, b] = work.tile([P, NL], F32, tag="res", bufs=8, name=f"res{c}_{b}")
+            nc.vector.tensor_tensor(
+                out=res[c, b][:], in0=lint[:, NI * c + i, cols], in1=z[c, b][:], op=SUB
+            )
+
+        def damp_and_store(c, b, engine):
+            i, l = divmod(b, 2)
+            row = NI * c + i
+            cols = slice(NL * l, NL * (l + 1))
+            engine.tensor_tensor(out=res[c, b][:], in0=res[c, b][:], in1=dampt[:, cols], op=MULT)
+            nc.sync.dma_start(out=out[P * row : P * (row + 1), cols], in_=res[c, b][:])
+
+        def finish(c, b):
+            subtract(c, b)
+            damp_and_store(c, b, nc.gpsimd)
+
+        permute_v(0)
+        field(0)
+        permute_v(1)
+        for n in range(STEPS):
+            if n < LAST:
+                field(n + 1)
+            for b in range(4):
+                c, r = divmod(n - 7 - b, JG)
+                if r == 0 and c >= 0:
+                    finish(c, b)
+            square(n, 0)
+            square(n, 1)
+            cube(n, 0)
+            cube(n, 1)
+            if n >= 1:
+                interleave(n - 1)
+            if n >= 2:
+                quantise(n - 2)
+            if n + 2 < JG:
+                permute_v(n + 2)
+            if n < LAST:
+                for b in range(4):
+                    if n - 3 - b >= 0:
+                        analyse(n - 3 - b, b)
+        interleave(LAST)
+        for n, b in ((11, 1), (10, 2), (11, 2), (9, 3), (10, 3), (11, 3), (12, 0)):
+            analyse(n, b)
+        quantise(14)
+        analyse(13, 0)
+        analyse(14, 0)
+        finish(2, 1)
+        for n in (12, 13, 14):
+            analyse(n, 1)
+        quantise(15)
+        analyse(15, 0)
+        analyse(15, 1)
+        for b in (2, 3):
+            finish(2, b)
+        for b in (2, 3):
+            for n in range(12, 16):
+                analyse(n, b)
+        finish(3, 0)
+        subtract(3, 1)
+        subtract(3, 2)
+        damp_and_store(3, 1, nc.vector)
+        subtract(3, 3)
+        damp_and_store(3, 2, nc.vector)
+        damp_and_store(3, 3, nc.vector)

@@ -20,12 +20,11 @@ K, M, L, R = 1024, 1024, 2048, 1024
 PACK = 4
 KG = 2
 JG = 4
-CH = 256
-NCH = M // CH
-NI = CH // P
+CH = 512
 NL = 512
-STEPS = NCH * JG
+STEPS = (M // CH) * JG
 LAST = STEPS - 1
+BANKS = 4
 
 
 def tile_phase_field_step_s4_kernel(
@@ -55,7 +54,7 @@ def tile_phase_field_step_s4_kernel(
         ctx.enter_context(tc.manual_schedule())
 
         nc.vector.memset(vsraw[:].rearrange("p g n -> p (g n)").bitcast(I32), 0)
-        nc.gpsimd.memset(asc[:].rearrange("p g n -> p (g n)").bitcast(I32), 0)
+        nc.vector.memset(asc[:].rearrange("p g n -> p (g n)").bitcast(I32), 0)
         nc.vector.memset(dummy[:], 0.0)
         nc.vector.memset(csc[:].bitcast(I32), 0)
 
@@ -66,9 +65,9 @@ def tile_phase_field_step_s4_kernel(
                     in_=v_scales[:, 4 * q : 4 * q + 4, :].rearrange("g r n -> r g n").bitcast(I32),
                 )
 
-        def load_v_words(lo, hi):
+        def load_v_words(lo, hi, engine):
             cols = slice(2 * lo, 2 * hi)
-            nc.sync.dma_start(
+            engine.dma_start(
                 out=vraw[:, :, cols].bitcast(I32),
                 in_=v_words.rearrange("g p b -> p g b")[:, :, cols].bitcast(I32),
             )
@@ -89,18 +88,18 @@ def tile_phase_field_step_s4_kernel(
         def load_lin(i):
             nc.sync.dma_start(out=lint[:, i, :], in_=lin[P * i : P * (i + 1), :])
 
-        load_v_words(0, 1024)
+        load_v_words(0, 512, nc.sync)
+        load_v_words(512, 1024, nc.gpsimd)
         load_v_scales()
         load_a_words(0, CH)
         for q in range(4):
-            engine = nc.scalar if q < 2 else nc.gpsimd
-            engine.dma_start(
+            nc.scalar.dma_start(
                 out=asc[32 * q : 32 * q + 4, :, :].bitcast(I32),
                 in_=a_scales[:, 4 * q : 4 * q + 4, :].rearrange("g r n -> r g n").bitcast(I32),
             )
         nc.scalar.activation(dummy[:, 1:2], dummy[:, 0:1], SQUARE)
         nc.gpsimd.dma_start(out=mobt[:], in_=mob.rearrange("(j p t) -> p j t", p=P, t=PACK))
-        load_v_words(1024, L)
+        load_v_words(1024, L, nc.sync)
         load_a_words(CH, M)
         load_c_words(0)
         for q in range(4):
@@ -136,136 +135,166 @@ def tile_phase_field_step_s4_kernel(
                 in_=vsraw[:, :, 512 * j : 512 * (j + 1)].rearrange("p g (m t) -> p g t m", t=PACK),
             )
 
-        def field(n):
+        def field(n, t):
             c, j = divmod(n, JG)
-            for h in range(2):
-                bank = psum.tile([P, 2, CH], F32, tag=f"u{h}", bufs=2, name=f"u{n}_{h}")
-                u[n, h] = bank
-                for e in range(2):
-                    t = 2 * h + e
-                    for g in range(KG):
-                        nc.tensor.matmul_mx(
-                            out=bank[:, e, :],
-                            lhsT=vw[j][:, g, t].rearrange("p m b -> p (m b)").bitcast(FP4X4),
-                            lhsT_scale=vs[j][:, g, t],
-                            rhs=aw[:, g, 2 * CH * c : 2 * CH * (c + 1)].bitcast(FP4X4),
-                            rhs_scale=asc[:, g, CH * c : CH * (c + 1)],
-                            start=(g == 0),
-                            stop=(g == KG - 1),
-                        )
-
-        def square(n, h):
-            sq[n, h] = work.tile([P, 2, CH], F32, tag="sq", name=f"sq{n}_{h}")
-            nc.scalar.activation(sq[n, h][:], u[n, h][:], SQUARE)
-
-        def cube(n, h):
-            j = n % JG
-            if h == 0:
-                ht[n] = work.tile([P, PACK, CH], BF16, tag="ht", name=f"ht{n}", align_bytes=64)
-            for e in range(2):
-                t = 2 * h + e
-                nc.vector.scalar_tensor_tensor(
-                    out=ht[n][:, t, :],
-                    in0=u[n, h][:, e, :],
-                    scalar=mobt[:, j, t : t + 1],
-                    in1=sq[n, h][:, e, :],
-                    op0=MULT,
-                    op1=MULT,
+            u[n, t] = psum.tile([P, CH], F32, tag=f"u{t}", bufs=1, name=f"u{n}_{t}")
+            for g in range(KG):
+                nc.tensor.matmul_mx(
+                    out=u[n, t][:],
+                    lhsT=vw[j][:, g, t].rearrange("p m b -> p (m b)").bitcast(FP4X4),
+                    lhsT_scale=vs[j][:, g, t],
+                    rhs=aw[:, g, 2 * CH * c : 2 * CH * (c + 1)].bitcast(FP4X4),
+                    rhs_scale=asc[:, g, CH * c : CH * (c + 1)],
+                    start=(g == 0),
+                    stop=(g == KG - 1),
                 )
 
-        def interleave(n):
-            hi[n] = work.tile([P, CH, PACK], BF16, tag="hi", name=f"hi{n}", align_bytes=64)
-            nc.scalar.copy(
-                hi[n][:].rearrange("p (c i) t -> p c t i", i=4),
-                ht[n][:].rearrange("p t (c i) -> p c t i", i=4),
+        def square(n, t):
+            sq[n, t] = work.tile([P, CH], F32, tag="sq", name=f"sq{n}_{t}")
+            nc.scalar.activation(sq[n, t][:], u[n, t][:], SQUARE)
+
+        def cube(n, t):
+            if t == 0:
+                ht[n] = work.tile([P, PACK, CH], BF16, tag="ht", bufs=3, name=f"ht{n}", align_bytes=64)
+            nc.vector.scalar_tensor_tensor(
+                out=ht[n][:, t, :],
+                in0=u[n, t][:],
+                scalar=mobt[:, n % JG, t : t + 1],
+                in1=sq[n, t][:],
+                op0=MULT,
+                op1=MULT,
             )
 
-        def quantise(n):
+        def interleave(n, p, engine):
+            if n not in hi:
+                hi[n] = work.tile([P, CH, PACK], BF16, tag="hi", bufs=3, name=f"hi{n}", align_bytes=64)
+            dst = hi[n][:, P * p : P * (p + 1), :].rearrange("p (c i) t -> p c t i", i=4)
+            src = ht[n][:, :, P * p : P * (p + 1)].rearrange("p t (c i) -> p c t i", i=4)
+            if engine == "s":
+                nc.scalar.copy(dst, src)
+            elif engine == "v":
+                nc.vector.tensor_copy(out=dst, in_=src)
+            else:
+                nc.gpsimd.tensor_scalar(
+                    out=dst, in0=src, scalar1=1.0, scalar2=0.0, op0=MULT, op1=mybir.AluOpType.add
+                )
+
+        def quantise(n, lo=0, hi_col=CH):
             nc.vector.quantize_mx(
-                out=hq[n][:].bitcast(FP8X4),
-                scales=hs[n][:],
-                in_=hi[n][:].rearrange("p n t -> p (n t)"),
+                out=hq[n][:, lo:hi_col].bitcast(FP8X4),
+                scales=hs[n][:, lo:hi_col],
+                in_=hi[n][:, lo:hi_col, :].rearrange("p n t -> p (n t)"),
             )
 
-        def analyse(n, b):
-            c, j = divmod(n, JG)
+        def analyse(c, g, b, j):
             i, l = divmod(b, 2)
+            n = JG * c + j
+            x0 = P * (2 * g + i)
             if j == 0:
-                z[c, b] = psum.tile([P, NL], F32, tag=f"z{b}", bufs=1, name=f"z{c}_{b}")
+                z[c, g, b] = psum.tile([P, NL], F32, tag=f"z{b}", bufs=1, name=f"z{c}_{g}_{b}")
             nc.tensor.matmul_mx(
-                out=z[c, b][:],
-                lhsT=hq[n][:, P * i : P * (i + 1)].bitcast(FP8X4),
-                lhsT_scale=hs[n][:, P * i : P * (i + 1)],
+                out=z[c, g, b][:],
+                lhsT=hq[n][:, x0 : x0 + P].bitcast(FP8X4),
+                lhsT_scale=hs[n][:, x0 : x0 + P],
                 rhs=cw[:, j, NL * l : NL * (l + 1)].bitcast(FP8X4),
                 rhs_scale=csc[4 * j : P, NL * l : NL * (l + 1)],
                 start=(j == 0),
                 stop=(j == JG - 1),
             )
 
-        def subtract(c, b):
+        def subtract(c, g, b):
             i, l = divmod(b, 2)
+            row = 4 * c + 2 * g + i
             cols = slice(NL * l, NL * (l + 1))
-            res[c, b] = work.tile([P, NL], F32, tag="res", bufs=8, name=f"res{c}_{b}")
+            res[c, g, b] = work.tile([P, NL], F32, tag="res", bufs=8, name=f"res{c}_{g}_{b}")
             nc.vector.tensor_tensor(
-                out=res[c, b][:], in0=lint[:, NI * c + i, cols], in1=z[c, b][:], op=SUB
+                out=res[c, g, b][:], in0=lint[:, row, cols], in1=z[c, g, b][:], op=SUB
             )
 
-        def damp_and_store(c, b, engine):
+        def damp_and_store(c, g, b, engine):
             i, l = divmod(b, 2)
-            row = NI * c + i
+            row = 4 * c + 2 * g + i
             cols = slice(NL * l, NL * (l + 1))
-            engine.tensor_tensor(out=res[c, b][:], in0=res[c, b][:], in1=dampt[:, cols], op=MULT)
-            nc.sync.dma_start(out=out[P * row : P * (row + 1), cols], in_=res[c, b][:])
+            r = res[c, g, b]
+            engine.tensor_tensor(out=r[:], in0=r[:], in1=dampt[:, cols], op=MULT)
+            nc.sync.dma_start(out=out[P * row : P * (row + 1), cols], in_=r[:])
 
-        def finish(c, b):
-            subtract(c, b)
-            damp_and_store(c, b, nc.gpsimd)
+        def finish(c, g, b):
+            subtract(c, g, b)
+            damp_and_store(c, g, b, nc.gpsimd)
 
+        movers = {1: "ssss", 2: "sgvs", 3: "sgvs", 4: "sgvs", 5: "ssss", 6: "ssss", 7: "ssss"}
         permute_v(0)
-        field(0)
+        for t in range(PACK):
+            field(0, t)
+        square(0, 0)
         permute_v(1)
         for n in range(STEPS):
-            if n < LAST:
-                field(n + 1)
-            for b in range(4):
-                c, r = divmod(n - 7 - b, JG)
-                if r == 0 and c >= 0:
-                    finish(c, b)
-            square(n, 0)
-            square(n, 1)
-            cube(n, 0)
-            cube(n, 1)
-            if n >= 1:
-                interleave(n - 1)
-            if n >= 2:
-                quantise(n - 2)
+            for t in range(PACK):
+                if n == 6 and t == 0:
+                    finish(0, 0, 2)
+                cube(n, t)
+                if n < LAST:
+                    field(n + 1, t)
+                if t + 1 < PACK:
+                    square(n, t + 1)
+                elif n < LAST:
+                    square(n + 1, 0)
+                if n >= 1:
+                    interleave(n - 1, t, movers[n][t])
+                if t == 1 and 2 <= n < LAST:
+                    quantise(n - 2)
+                if 2 <= n <= 4:
+                    if t == 2:
+                        analyse(0, 0, 0, n - 2)
+                        analyse(0, 0, 1, n - 2)
+                    if t == 3:
+                        analyse(0, 0, 2, n - 2)
+                        analyse(0, 0, 3, n - 2)
+                if n == 5:
+                    if t == 1:
+                        for b in range(BANKS):
+                            analyse(0, 0, b, 3)
+                    if t >= 2:
+                        finish(0, 0, t - 2)
+                        for j in range(JG):
+                            analyse(0, 1, t - 2, j)
+                if n == 6:
+                    if t == 0:
+                        for j in range(JG):
+                            analyse(0, 1, 2, j)
+                    if t == 1:
+                        finish(0, 0, 3)
+                        for j in range(JG):
+                            analyse(0, 1, 3, j)
+                    if t >= 2:
+                        finish(0, 1, t - 2)
+                        analyse(1, 0, t - 2, 0)
+                if n == 7 and t < 2:
+                    finish(0, 1, t + 2)
+                    analyse(1, 0, t + 2, 0)
             if n + 2 < JG:
                 permute_v(n + 2)
-            if n < LAST:
-                for b in range(4):
-                    if n - 3 - b >= 0:
-                        analyse(n - 3 - b, b)
-        interleave(LAST)
-        for n, b in ((11, 1), (10, 2), (11, 2), (9, 3), (10, 3), (11, 3), (12, 0)):
-            analyse(n, b)
-        quantise(14)
-        analyse(13, 0)
-        analyse(14, 0)
-        finish(2, 1)
-        for n in (12, 13, 14):
-            analyse(n, 1)
-        quantise(15)
-        analyse(15, 0)
-        analyse(15, 1)
-        for b in (2, 3):
-            finish(2, b)
-        for b in (2, 3):
-            for n in range(12, 16):
-                analyse(n, b)
-        finish(3, 0)
-        subtract(3, 1)
-        subtract(3, 2)
-        damp_and_store(3, 1, nc.vector)
-        subtract(3, 3)
-        damp_and_store(3, 2, nc.vector)
-        damp_and_store(3, 3, nc.vector)
+        quantise(LAST - 2)
+        for b in range(BANKS):
+            analyse(1, 0, b, 1)
+        interleave(LAST, 0, "v")
+        interleave(LAST, 1, "v")
+        interleave(LAST, 2, "s")
+        interleave(LAST, 3, "s")
+        quantise(LAST, 0, CH // 2)
+        quantise(LAST - 1)
+        quantise(LAST, CH // 2, CH)
+        for b in range(BANKS):
+            analyse(1, 0, b, 2)
+            analyse(1, 0, b, 3)
+        for b in range(BANKS):
+            finish(1, 0, b)
+        for b in range(BANKS):
+            for j in range(JG):
+                analyse(1, 1, b, j)
+        subtract(1, 1, 0)
+        for b in range(1, BANKS):
+            subtract(1, 1, b)
+            damp_and_store(1, 1, b - 1, nc.vector)
+        damp_and_store(1, 1, 3, nc.vector)

@@ -51,10 +51,8 @@ def tile_phase_field_step_s4_kernel(
         hq = [keep.tile([P, CH], U32, name=f"hq{n}", align_bytes=64) for n in range(STEPS)]
         hs = [keep.tile([P, CH], U8, name=f"hs{n}", align_bytes=64) for n in range(STEPS)]
 
-        ctx.enter_context(tc.manual_schedule())
-
-        nc.vector.memset(vsraw[:].rearrange("p g n -> p (g n)").bitcast(I32), 0)
         nc.vector.memset(asc[:].rearrange("p g n -> p (g n)").bitcast(I32), 0)
+        nc.vector.memset(vsraw[:].rearrange("p g n -> p (g n)").bitcast(I32), 0)
         nc.vector.memset(dummy[:], 0.0)
         nc.vector.memset(csc[:].bitcast(I32), 0)
 
@@ -72,9 +70,9 @@ def tile_phase_field_step_s4_kernel(
                 in_=v_words.rearrange("g p b -> p g b")[:, :, cols].bitcast(I32),
             )
 
-        def load_a_words(lo, hi):
+        def load_a_words(lo, hi, engine):
             cols = slice(2 * lo, 2 * hi)
-            nc.sync.dma_start(
+            engine.dma_start(
                 out=aw[:, :, cols].bitcast(I32),
                 in_=a_words.rearrange("g p b -> p g b")[:, :, cols].bitcast(I32),
             )
@@ -89,18 +87,19 @@ def tile_phase_field_step_s4_kernel(
             nc.sync.dma_start(out=lint[:, i, :], in_=lin[P * i : P * (i + 1), :])
 
         load_v_words(0, 512, nc.sync)
-        load_v_words(512, 1024, nc.gpsimd)
+        load_a_words(0, CH, nc.gpsimd)
         load_v_scales()
-        load_a_words(0, CH)
         for q in range(4):
-            nc.scalar.dma_start(
+            engine = nc.scalar if q < 3 else nc.gpsimd
+            engine.dma_start(
                 out=asc[32 * q : 32 * q + 4, :, :].bitcast(I32),
                 in_=a_scales[:, 4 * q : 4 * q + 4, :].rearrange("g r n -> r g n").bitcast(I32),
             )
         nc.scalar.activation(dummy[:, 1:2], dummy[:, 0:1], SQUARE)
         nc.gpsimd.dma_start(out=mobt[:], in_=mob.rearrange("(j p t) -> p j t", p=P, t=PACK))
+        load_v_words(512, 1024, nc.sync)
         load_v_words(1024, L, nc.sync)
-        load_a_words(CH, M)
+        load_a_words(CH, M, nc.sync)
         load_c_words(0)
         for q in range(4):
             nc.sync.dma_start(
@@ -223,7 +222,7 @@ def tile_phase_field_step_s4_kernel(
             subtract(c, g, b)
             damp_and_store(c, g, b, nc.gpsimd)
 
-        movers = {1: "ssss", 2: "sgvs", 3: "sgvs", 4: "sgvs", 5: "ssss", 6: "ssss", 7: "ssss"}
+        movers = {1: "ssss", 2: "svvs", 3: "svvs", 4: "svvs", 5: "ssss", 6: "ssss", 7: "ssss"}
         permute_v(0)
         for t in range(PACK):
             field(0, t)
@@ -278,7 +277,7 @@ def tile_phase_field_step_s4_kernel(
         quantise(LAST - 2)
         for b in range(BANKS):
             analyse(1, 0, b, 1)
-        interleave(LAST, 0, "v")
+        interleave(LAST, 0, "s")
         interleave(LAST, 1, "v")
         interleave(LAST, 2, "s")
         interleave(LAST, 3, "s")

@@ -2,7 +2,20 @@ from contextlib import ExitStack
 
 import concourse.mybir as mybir
 
-FLOPS = 2 * 1024 * 1024 * 2048 * 2
+P = 128
+K, M, L, R = 1024, 1024, 2048, 1024
+PACK = 4
+K_PASS = P * PACK
+KG = K // K_PASS
+JG = L // K_PASS
+CH = 512
+NL = 512
+PIECES = CH // P
+STEPS = (M // CH) * JG
+LAST = STEPS - 1
+BANKS = 4
+
+FLOPS = 2 * K * M * L + 2 * L * M * R
 
 F32 = mybir.dt.float32
 BF16 = mybir.dt.bfloat16
@@ -12,19 +25,8 @@ U8 = mybir.dt.uint8
 FP4X4 = mybir.dt.float4_e2m1fn_x4
 FP8X4 = mybir.dt.float8_e4m3fn_x4
 MULT = mybir.AluOpType.mult
-SUB = mybir.AluOpType.subtract
+SUBTRACT = mybir.AluOpType.subtract
 SQUARE = mybir.ActivationFunctionType.Square
-
-P = 128
-K, M, L, R = 1024, 1024, 2048, 1024
-PACK = 4
-KG = 2
-JG = 4
-CH = 512
-NL = 512
-STEPS = (M // CH) * JG
-LAST = STEPS - 1
-BANKS = 4
 
 
 def tile_phase_field_step_s4_kernel(
@@ -36,193 +38,222 @@ def tile_phase_field_step_s4_kernel(
         work = ctx.enter_context(tc.tile_pool(name="work", bufs=4))
         psum = ctx.enter_context(tc.psum_pool(name="psum", bufs=2))
 
-        vraw = keep.tile([P, KG, 2 * L], U8, name="vraw", align_bytes=64)
-        vsraw = keep.tile([P, KG, L], U8, name="vsraw", align_bytes=64)
-        vw = [keep.tile([P, KG, PACK, P, 2], U8, name=f"vw{j}", align_bytes=64) for j in range(JG)]
-        vs = [keep.tile([P, KG, PACK, P], U8, name=f"vs{j}", align_bytes=64) for j in range(JG)]
-        aw = keep.tile([P, KG, 2 * M], U8, name="aw", align_bytes=64)
-        asc = keep.tile([P, KG, M], U8, name="asc", align_bytes=64)
-        cw = keep.tile([P, JG, R], U32, name="cw", align_bytes=64)
-        csc = keep.tile([P, R], U8, name="csc", align_bytes=64)
-        mobt = keep.tile([P, JG, PACK], BF16, name="mobt")
-        lint = keep.tile([P, M // P, R], BF16, name="lint")
-        dampt = keep.tile([P, R], BF16, name="dampt")
+        v_raw = keep.tile([P, KG, 2 * L], U8, name="v_raw", align_bytes=64)
+        v_raw_scales = [
+            keep.tile([P, KG, L // 2], U8, name=f"v_raw_scales{i}", align_bytes=64) for i in range(2)
+        ]
+        v_codes = [keep.tile([P, KG, PACK, P, 2], U8, name=f"v_codes{j}", align_bytes=64) for j in range(JG)]
+        v_planes = [keep.tile([P, KG, PACK, P], U8, name=f"v_planes{j}", align_bytes=64) for j in range(JG)]
+        a_codes = keep.tile([P, KG, 2 * M], U8, name="a_codes", align_bytes=64)
+        a_planes = keep.tile([P, KG, M], U8, name="a_planes", align_bytes=64)
+        c_codes = keep.tile([P, JG, R], U32, name="c_codes", align_bytes=64)
+        c_planes = keep.tile([P, R], U8, name="c_planes", align_bytes=64)
+        mob_cols = keep.tile([P, JG, PACK], BF16, name="mob_cols")
+        lin_rows = keep.tile([P, M // P, R], BF16, name="lin_rows")
+        damp_rows = keep.tile([P, R], BF16, name="damp_rows")
         dummy = keep.tile([P, 2], F32, name="dummy")
-        hq = [keep.tile([P, CH], U32, name=f"hq{n}", align_bytes=64) for n in range(STEPS)]
-        hs = [keep.tile([P, CH], U8, name=f"hs{n}", align_bytes=64) for n in range(STEPS)]
+        h_codes = [keep.tile([P, CH], U32, name=f"h_codes{n}", align_bytes=64) for n in range(STEPS)]
+        h_planes = [keep.tile([P, CH], U8, name=f"h_planes{n}", align_bytes=64) for n in range(STEPS)]
 
-        nc.vector.memset(asc[:].rearrange("p g n -> p (g n)").bitcast(I32), 0)
-        nc.vector.memset(vsraw[:].rearrange("p g n -> p (g n)").bitcast(I32), 0)
+        nc.vector.memset(a_planes[:].rearrange("p g n -> p (g n)").bitcast(I32), 0)
+        nc.vector.memset(v_raw_scales[0][:].rearrange("p g n -> p (g n)").bitcast(I32), 0)
         nc.vector.memset(dummy[:], 0.0)
-        nc.vector.memset(csc[:].bitcast(I32), 0)
+        nc.vector.memset(v_raw_scales[1][:].rearrange("p g n -> p (g n)").bitcast(I32), 0)
+        nc.vector.memset(c_planes[:].bitcast(I32), 0)
 
-        def load_v_scales():
-            for q in range(4):
-                nc.sync.dma_start(
-                    out=vsraw[32 * q : 32 * q + 4, :, :].bitcast(I32),
-                    in_=v_scales[:, 4 * q : 4 * q + 4, :].rearrange("g r n -> r g n").bitcast(I32),
-                )
-
-        def load_v_words(lo, hi, engine):
+        def load_v_words(lo, hi):
             cols = slice(2 * lo, 2 * hi)
-            engine.dma_start(
-                out=vraw[:, :, cols].bitcast(I32),
+            nc.sync.dma_start(
+                out=v_raw[:, :, cols].bitcast(I32),
                 in_=v_words.rearrange("g p b -> p g b")[:, :, cols].bitcast(I32),
             )
 
-        def load_a_words(lo, hi, engine):
+        def load_v_scales(i):
+            cols = slice(L // 2 * i, L // 2 * (i + 1))
+            for q in range(4):
+                nc.sync.dma_start(
+                    out=v_raw_scales[i][32 * q : 32 * q + 4, :, :].bitcast(I32),
+                    in_=v_scales[:, 4 * q : 4 * q + 4, cols].rearrange("g r n -> r g n").bitcast(I32),
+                )
+
+        def load_a_words(lo, hi):
             cols = slice(2 * lo, 2 * hi)
-            engine.dma_start(
-                out=aw[:, :, cols].bitcast(I32),
+            nc.sync.dma_start(
+                out=a_codes[:, :, cols].bitcast(I32),
                 in_=a_words.rearrange("g p b -> p g b")[:, :, cols].bitcast(I32),
             )
 
-        def load_c_words(g):
-            nc.sync.dma_start(
-                out=cw[:, g, :].bitcast(I32),
-                in_=c_words[g].rearrange("p n t -> p (n t)").bitcast(I32),
-            )
-
-        def load_lin(i):
-            nc.sync.dma_start(out=lint[:, i, :], in_=lin[P * i : P * (i + 1), :])
-
-        load_v_words(0, 512, nc.sync)
-        load_a_words(0, CH, nc.gpsimd)
-        load_v_scales()
-        for q in range(4):
-            engine = nc.scalar if q < 3 else nc.gpsimd
-            engine.dma_start(
-                out=asc[32 * q : 32 * q + 4, :, :].bitcast(I32),
+        def load_a_scales(q):
+            nc.scalar.dma_start(
+                out=a_planes[32 * q : 32 * q + 4, :, :].bitcast(I32),
                 in_=a_scales[:, 4 * q : 4 * q + 4, :].rearrange("g r n -> r g n").bitcast(I32),
             )
+
+        def load_c_words(j):
+            nc.sync.dma_start(
+                out=c_codes[:, j, :].bitcast(I32),
+                in_=c_words[j].rearrange("p n t -> p (n t)").bitcast(I32),
+            )
+
+        def load_lin(row):
+            nc.sync.dma_start(out=lin_rows[:, row, :], in_=lin[P * row : P * (row + 1), :])
+
+        load_v_words(0, K_PASS)
+        load_v_scales(0)
+        for q in range(3):
+            load_a_scales(q)
         nc.scalar.activation(dummy[:, 1:2], dummy[:, 0:1], SQUARE)
-        nc.gpsimd.dma_start(out=mobt[:], in_=mob.rearrange("(j p t) -> p j t", p=P, t=PACK))
-        load_v_words(512, 1024, nc.sync)
-        load_v_words(1024, L, nc.sync)
-        load_a_words(CH, M, nc.sync)
+        load_a_words(0, CH)
+        load_a_scales(3)
+        nc.scalar.dma_start(out=mob_cols[:], in_=mob.rearrange("(j p t) -> p j t", p=P, t=PACK))
+        load_v_words(K_PASS, 2 * K_PASS)
+        load_v_scales(1)
+        load_v_words(2 * K_PASS, L)
+        load_a_words(CH, M)
         load_c_words(0)
         for q in range(4):
             nc.sync.dma_start(
-                out=csc[32 * q : 32 * q + 16, :].bitcast(I32),
+                out=c_planes[32 * q : 32 * q + 16, :].bitcast(I32),
                 in_=c_scales[:, 4 * q : 4 * q + 4, :].bitcast(I32),
             )
-        load_c_words(1)
-        load_c_words(2)
-        load_c_words(3)
-        load_lin(0)
-        load_lin(1)
-        nc.sync.dma_start(out=dampt[:], in_=damp.partition_broadcast(P))
-        for i in range(2, M // P):
-            load_lin(i)
+        for j in range(1, JG):
+            load_c_words(j)
+        for row in range(2):
+            load_lin(row)
+        nc.sync.dma_start(out=damp_rows[:], in_=damp.partition_broadcast(P))
+        for row in range(2, M // P):
+            load_lin(row)
 
-        u = {}
-        sq = {}
-        ht = {}
-        hi = {}
-        z = {}
-        res = {}
+        u, squares, h_by_t, h_packed, z, res = {}, {}, {}, {}, {}, {}
 
         def permute_v(j):
-            for g in range(KG):
-                cols = slice(1024 * j, 1024 * (j + 1))
+            cols = slice(2 * K_PASS * j, 2 * K_PASS * (j + 1))
+            for kg in range(KG):
                 nc.vector.tensor_copy(
-                    out=vw[j][:, g],
-                    in_=vraw[:, g, cols].rearrange("p (m t b) -> p t m b", t=PACK, b=2),
+                    out=v_codes[j][:, kg],
+                    in_=v_raw[:, kg, cols].rearrange("p (m t b) -> p t m b", t=PACK, b=2),
                 )
+            half, first = divmod(K_PASS * j, L // 2)
             nc.vector.tensor_copy(
-                out=vs[j][:],
-                in_=vsraw[:, :, 512 * j : 512 * (j + 1)].rearrange("p g (m t) -> p g t m", t=PACK),
+                out=v_planes[j][:],
+                in_=v_raw_scales[half][:, :, first : first + K_PASS].rearrange("p g (m t) -> p g t m", t=PACK),
             )
 
         def field(n, t):
             c, j = divmod(n, JG)
             u[n, t] = psum.tile([P, CH], F32, tag=f"u{t}", bufs=1, name=f"u{n}_{t}")
-            for g in range(KG):
+            for kg in range(KG):
                 nc.tensor.matmul_mx(
                     out=u[n, t][:],
-                    lhsT=vw[j][:, g, t].rearrange("p m b -> p (m b)").bitcast(FP4X4),
-                    lhsT_scale=vs[j][:, g, t],
-                    rhs=aw[:, g, 2 * CH * c : 2 * CH * (c + 1)].bitcast(FP4X4),
-                    rhs_scale=asc[:, g, CH * c : CH * (c + 1)],
-                    start=(g == 0),
-                    stop=(g == KG - 1),
+                    lhsT=v_codes[j][:, kg, t].rearrange("p m b -> p (m b)").bitcast(FP4X4),
+                    lhsT_scale=v_planes[j][:, kg, t],
+                    rhs=a_codes[:, kg, 2 * CH * c : 2 * CH * (c + 1)].bitcast(FP4X4),
+                    rhs_scale=a_planes[:, kg, CH * c : CH * (c + 1)],
+                    start=(kg == 0),
+                    stop=(kg == KG - 1),
                 )
 
         def square(n, t):
-            sq[n, t] = work.tile([P, CH], F32, tag="sq", name=f"sq{n}_{t}")
-            nc.scalar.activation(sq[n, t][:], u[n, t][:], SQUARE)
+            squares[n, t] = work.tile([P, CH], F32, tag="squares", name=f"squares{n}_{t}")
+            nc.scalar.activation(squares[n, t][:], u[n, t][:], SQUARE)
 
         def cube(n, t):
             if t == 0:
-                ht[n] = work.tile([P, PACK, CH], BF16, tag="ht", bufs=3, name=f"ht{n}", align_bytes=64)
+                h_by_t[n] = work.tile(
+                    [P, PACK, CH], BF16, tag="h_by_t", bufs=3, name=f"h_by_t{n}", align_bytes=64
+                )
             nc.vector.scalar_tensor_tensor(
-                out=ht[n][:, t, :],
+                out=h_by_t[n][:, t, :],
                 in0=u[n, t][:],
-                scalar=mobt[:, n % JG, t : t + 1],
-                in1=sq[n, t][:],
+                scalar=mob_cols[:, n % JG, t : t + 1],
+                in1=squares[n, t][:],
                 op0=MULT,
                 op1=MULT,
             )
 
-        def interleave(n, p, engine):
-            if n not in hi:
-                hi[n] = work.tile([P, CH, PACK], BF16, tag="hi", bufs=3, name=f"hi{n}", align_bytes=64)
-            dst = hi[n][:, P * p : P * (p + 1), :].rearrange("p (c i) t -> p c t i", i=4)
-            src = ht[n][:, :, P * p : P * (p + 1)].rearrange("p t (c i) -> p c t i", i=4)
-            if engine == "s":
-                nc.scalar.copy(dst, src)
-            elif engine == "v":
-                nc.vector.tensor_copy(out=dst, in_=src)
-            else:
-                nc.gpsimd.tensor_scalar(
-                    out=dst, in0=src, scalar1=1.0, scalar2=0.0, op0=MULT, op1=mybir.AluOpType.add
+        def interleave(n, piece, engine):
+            if n not in h_packed:
+                h_packed[n] = work.tile(
+                    [P, CH, PACK], BF16, tag="h_packed", bufs=3, name=f"h_packed{n}", align_bytes=64
                 )
+            x = slice(P * piece, P * (piece + 1))
+            dst = h_packed[n][:, x, :].rearrange("p (c i) t -> p c t i", i=4)
+            src = h_by_t[n][:, :, x].rearrange("p t (c i) -> p c t i", i=4)
+            if engine == "scalar":
+                nc.scalar.copy(dst, src)
+            else:
+                nc.vector.tensor_copy(out=dst, in_=src)
 
-        def quantise(n, lo=0, hi_col=CH):
+        def quantise(n, lo=0, hi=CH):
             nc.vector.quantize_mx(
-                out=hq[n][:, lo:hi_col].bitcast(FP8X4),
-                scales=hs[n][:, lo:hi_col],
-                in_=hi[n][:, lo:hi_col, :].rearrange("p n t -> p (n t)"),
+                out=h_codes[n][:, lo:hi].bitcast(FP8X4),
+                scales=h_planes[n][:, lo:hi],
+                in_=h_packed[n][:, lo:hi, :].rearrange("p n t -> p (n t)"),
             )
 
-        def analyse(c, g, b, j):
-            i, l = divmod(b, 2)
+        def place(c, pair, b):
+            i, half = divmod(b, 2)
+            return (CH // P) * c + 2 * pair + i, slice(NL * half, NL * (half + 1))
+
+        def analyse(c, pair, b, j):
+            row, cols = place(c, pair, b)
             n = JG * c + j
-            x0 = P * (2 * g + i)
+            x = slice(P * row - CH * c, P * (row + 1) - CH * c)
             if j == 0:
-                z[c, g, b] = psum.tile([P, NL], F32, tag=f"z{b}", bufs=1, name=f"z{c}_{g}_{b}")
+                z[c, pair, b] = psum.tile([P, NL], F32, tag=f"z{b}", bufs=1, name=f"z{c}_{pair}_{b}")
             nc.tensor.matmul_mx(
-                out=z[c, g, b][:],
-                lhsT=hq[n][:, x0 : x0 + P].bitcast(FP8X4),
-                lhsT_scale=hs[n][:, x0 : x0 + P],
-                rhs=cw[:, j, NL * l : NL * (l + 1)].bitcast(FP8X4),
-                rhs_scale=csc[4 * j : P, NL * l : NL * (l + 1)],
+                out=z[c, pair, b][:],
+                lhsT=h_codes[n][:, x].bitcast(FP8X4),
+                lhsT_scale=h_planes[n][:, x],
+                rhs=c_codes[:, j, cols].bitcast(FP8X4),
+                rhs_scale=c_planes[4 * j : P, cols],
                 start=(j == 0),
                 stop=(j == JG - 1),
             )
 
-        def subtract(c, g, b):
-            i, l = divmod(b, 2)
-            row = 4 * c + 2 * g + i
-            cols = slice(NL * l, NL * (l + 1))
-            res[c, g, b] = work.tile([P, NL], F32, tag="res", bufs=8, name=f"res{c}_{g}_{b}")
+        def subtract(c, pair, b):
+            row, cols = place(c, pair, b)
+            res[c, pair, b] = work.tile([P, NL], F32, tag="res", bufs=8, name=f"res{c}_{pair}_{b}")
             nc.vector.tensor_tensor(
-                out=res[c, g, b][:], in0=lint[:, row, cols], in1=z[c, g, b][:], op=SUB
+                out=res[c, pair, b][:], in0=lin_rows[:, row, cols], in1=z[c, pair, b][:], op=SUBTRACT
             )
 
-        def damp_and_store(c, g, b, engine):
-            i, l = divmod(b, 2)
-            row = 4 * c + 2 * g + i
-            cols = slice(NL * l, NL * (l + 1))
-            r = res[c, g, b]
-            engine.tensor_tensor(out=r[:], in0=r[:], in1=dampt[:, cols], op=MULT)
+        def damp_and_store(c, pair, b, engine):
+            row, cols = place(c, pair, b)
+            r = res[c, pair, b]
+            engine.tensor_tensor(out=r[:], in0=r[:], in1=damp_rows[:, cols], op=MULT)
             nc.sync.dma_start(out=out[P * row : P * (row + 1), cols], in_=r[:])
 
-        def finish(c, g, b):
-            subtract(c, g, b)
-            damp_and_store(c, g, b, nc.gpsimd)
+        def finish(c, pair, b):
+            subtract(c, pair, b)
+            damp_and_store(c, pair, b, nc.gpsimd)
 
-        movers = {1: "ssss", 2: "svvs", 3: "svvs", 4: "svvs", 5: "ssss", 6: "ssss", 7: "ssss"}
+        def analyse_all_groups(c, pair, b):
+            for j in range(JG):
+                analyse(c, pair, b, j)
+
+        def second_product(n, t):
+            if 2 <= n <= 4 and t >= 2:
+                for b in (2 * t - 4, 2 * t - 3):
+                    analyse(0, 0, b, n - 2)
+            if n == 5 and t == 1:
+                for b in range(BANKS):
+                    analyse(0, 0, b, JG - 1)
+            if n == 5 and t >= 2:
+                finish(0, 0, t - 2)
+                analyse_all_groups(0, 1, t - 2)
+            if n == 6 and t == 0:
+                analyse_all_groups(0, 1, 2)
+            if n == 6 and t == 1:
+                finish(0, 0, 3)
+                analyse_all_groups(0, 1, 3)
+            if n == 6 and t >= 2:
+                finish(0, 1, t - 2)
+                analyse(1, 0, t - 2, 0)
+            if n == 7 and t < 2:
+                finish(0, 1, t + 2)
+                analyse(1, 0, t + 2, 0)
+
         permute_v(0)
         for t in range(PACK):
             field(0, t)
@@ -240,47 +271,19 @@ def tile_phase_field_step_s4_kernel(
                 elif n < LAST:
                     square(n + 1, 0)
                 if n >= 1:
-                    interleave(n - 1, t, movers[n][t])
+                    mover = "vector" if 2 <= n <= 4 and 1 <= t <= 2 else "scalar"
+                    interleave(n - 1, t, mover)
                 if t == 1 and 2 <= n < LAST:
                     quantise(n - 2)
-                if 2 <= n <= 4:
-                    if t == 2:
-                        analyse(0, 0, 0, n - 2)
-                        analyse(0, 0, 1, n - 2)
-                    if t == 3:
-                        analyse(0, 0, 2, n - 2)
-                        analyse(0, 0, 3, n - 2)
-                if n == 5:
-                    if t == 1:
-                        for b in range(BANKS):
-                            analyse(0, 0, b, 3)
-                    if t >= 2:
-                        finish(0, 0, t - 2)
-                        for j in range(JG):
-                            analyse(0, 1, t - 2, j)
-                if n == 6:
-                    if t == 0:
-                        for j in range(JG):
-                            analyse(0, 1, 2, j)
-                    if t == 1:
-                        finish(0, 0, 3)
-                        for j in range(JG):
-                            analyse(0, 1, 3, j)
-                    if t >= 2:
-                        finish(0, 1, t - 2)
-                        analyse(1, 0, t - 2, 0)
-                if n == 7 and t < 2:
-                    finish(0, 1, t + 2)
-                    analyse(1, 0, t + 2, 0)
+                second_product(n, t)
             if n + 2 < JG:
                 permute_v(n + 2)
+
         quantise(LAST - 2)
         for b in range(BANKS):
             analyse(1, 0, b, 1)
-        interleave(LAST, 0, "s")
-        interleave(LAST, 1, "v")
-        interleave(LAST, 2, "s")
-        interleave(LAST, 3, "s")
+        for piece in range(PIECES):
+            interleave(LAST, piece, "vector" if piece == 1 else "scalar")
         quantise(LAST, 0, CH // 2)
         quantise(LAST - 1)
         quantise(LAST, CH // 2, CH)
@@ -290,10 +293,9 @@ def tile_phase_field_step_s4_kernel(
         for b in range(BANKS):
             finish(1, 0, b)
         for b in range(BANKS):
-            for j in range(JG):
-                analyse(1, 1, b, j)
+            analyse_all_groups(1, 1, b)
         subtract(1, 1, 0)
         for b in range(1, BANKS):
             subtract(1, 1, b)
             damp_and_store(1, 1, b - 1, nc.vector)
-        damp_and_store(1, 1, 3, nc.vector)
+        damp_and_store(1, 1, BANKS - 1, nc.vector)

from contextlib import ExitStack

import concourse.mybir as mybir

P = 128
K, M, L, R = 1024, 1024, 2048, 1024
PACK = 4
K_PASS = P * PACK
KG = K // K_PASS
JG = L // K_PASS
CH = 512
NL = 512
PIECES = CH // P
STEPS = (M // CH) * JG
LAST = STEPS - 1
BANKS = 4

FLOPS = 2 * K * M * L + 2 * L * M * R

F32 = mybir.dt.float32
BF16 = mybir.dt.bfloat16
I32 = mybir.dt.int32
U32 = mybir.dt.uint32
U8 = mybir.dt.uint8
FP4X4 = mybir.dt.float4_e2m1fn_x4
FP8X4 = mybir.dt.float8_e4m3fn_x4
MULT = mybir.AluOpType.mult
SUBTRACT = mybir.AluOpType.subtract
SQUARE = mybir.ActivationFunctionType.Square


def tile_phase_field_step_s4_kernel(
    tc, a_words, a_scales, v_words, v_scales, mob, c_words, c_scales, lin, damp, out
):
    nc = tc.nc
    with ExitStack() as ctx:
        keep = ctx.enter_context(tc.tile_pool(name="keep", bufs=1))
        work = ctx.enter_context(tc.tile_pool(name="work", bufs=4))
        psum = ctx.enter_context(tc.psum_pool(name="psum", bufs=2))

        v_raw = keep.tile([P, KG, 2 * L], U8, name="v_raw", align_bytes=64)
        v_raw_scales = [
            keep.tile([P, KG, L // 2], U8, name=f"v_raw_scales{i}", align_bytes=64) for i in range(2)
        ]
        v_codes = [keep.tile([P, KG, PACK, P, 2], U8, name=f"v_codes{j}", align_bytes=64) for j in range(JG)]
        v_planes = [keep.tile([P, KG, PACK, P], U8, name=f"v_planes{j}", align_bytes=64) for j in range(JG)]
        a_codes = keep.tile([P, KG, 2 * M], U8, name="a_codes", align_bytes=64)
        a_planes = keep.tile([P, KG, M], U8, name="a_planes", align_bytes=64)
        c_codes = keep.tile([P, JG, R], U32, name="c_codes", align_bytes=64)
        c_planes = keep.tile([P, R], U8, name="c_planes", align_bytes=64)
        mob_cols = keep.tile([P, JG, PACK], BF16, name="mob_cols")
        lin_rows = keep.tile([P, M // P, R], BF16, name="lin_rows")
        damp_rows = keep.tile([P, R], BF16, name="damp_rows")
        dummy = keep.tile([P, 2], F32, name="dummy")
        h_codes = [keep.tile([P, CH], U32, name=f"h_codes{n}", align_bytes=64) for n in range(STEPS)]
        h_planes = [keep.tile([P, CH], U8, name=f"h_planes{n}", align_bytes=64) for n in range(STEPS)]

        nc.vector.memset(a_planes[:].rearrange("p g n -> p (g n)").bitcast(I32), 0)
        nc.vector.memset(v_raw_scales[0][:].rearrange("p g n -> p (g n)").bitcast(I32), 0)
        nc.vector.memset(dummy[:], 0.0)
        nc.vector.memset(v_raw_scales[1][:].rearrange("p g n -> p (g n)").bitcast(I32), 0)
        nc.vector.memset(c_planes[:].bitcast(I32), 0)

        def load_v_words(lo, hi):
            cols = slice(2 * lo, 2 * hi)
            nc.sync.dma_start(
                out=v_raw[:, :, cols].bitcast(I32),
                in_=v_words.rearrange("g p b -> p g b")[:, :, cols].bitcast(I32),
            )

        def load_v_scales(i):
            cols = slice(L // 2 * i, L // 2 * (i + 1))
            for q in range(4):
                nc.sync.dma_start(
                    out=v_raw_scales[i][32 * q : 32 * q + 4, :, :].bitcast(I32),
                    in_=v_scales[:, 4 * q : 4 * q + 4, cols].rearrange("g r n -> r g n").bitcast(I32),
                )

        def load_a_words(lo, hi):
            cols = slice(2 * lo, 2 * hi)
            nc.sync.dma_start(
                out=a_codes[:, :, cols].bitcast(I32),
                in_=a_words.rearrange("g p b -> p g b")[:, :, cols].bitcast(I32),
            )

        def load_a_scales(q):
            nc.scalar.dma_start(
                out=a_planes[32 * q : 32 * q + 4, :, :].bitcast(I32),
                in_=a_scales[:, 4 * q : 4 * q + 4, :].rearrange("g r n -> r g n").bitcast(I32),
            )

        def load_c_words(j):
            nc.sync.dma_start(
                out=c_codes[:, j, :].bitcast(I32),
                in_=c_words[j].rearrange("p n t -> p (n t)").bitcast(I32),
            )

        def load_lin(row):
            nc.sync.dma_start(out=lin_rows[:, row, :], in_=lin[P * row : P * (row + 1), :])

        load_v_words(0, K_PASS)
        load_v_scales(0)
        for q in range(3):
            load_a_scales(q)
        nc.scalar.activation(dummy[:, 1:2], dummy[:, 0:1], SQUARE)
        load_a_words(0, CH)
        load_a_scales(3)
        nc.scalar.dma_start(out=mob_cols[:], in_=mob.rearrange("(j p t) -> p j t", p=P, t=PACK))
        load_v_words(K_PASS, 2 * K_PASS)
        load_v_scales(1)
        load_v_words(2 * K_PASS, L)
        load_a_words(CH, M)
        load_c_words(0)
        for q in range(4):
            nc.sync.dma_start(
                out=c_planes[32 * q : 32 * q + 16, :].bitcast(I32),
                in_=c_scales[:, 4 * q : 4 * q + 4, :].bitcast(I32),
            )
        for j in range(1, JG):
            load_c_words(j)
        for row in range(2):
            load_lin(row)
        nc.sync.dma_start(out=damp_rows[:], in_=damp.partition_broadcast(P))
        for row in range(2, M // P):
            load_lin(row)

        u, squares, h_by_t, h_packed, z, res = {}, {}, {}, {}, {}, {}

        def permute_v(j):
            cols = slice(2 * K_PASS * j, 2 * K_PASS * (j + 1))
            for kg in range(KG):
                nc.vector.tensor_copy(
                    out=v_codes[j][:, kg],
                    in_=v_raw[:, kg, cols].rearrange("p (m t b) -> p t m b", t=PACK, b=2),
                )
            half, first = divmod(K_PASS * j, L // 2)
            nc.vector.tensor_copy(
                out=v_planes[j][:],
                in_=v_raw_scales[half][:, :, first : first + K_PASS].rearrange("p g (m t) -> p g t m", t=PACK),
            )

        def field(n, t):
            c, j = divmod(n, JG)
            u[n, t] = psum.tile([P, CH], F32, tag=f"u{t}", bufs=1, name=f"u{n}_{t}")
            for kg in range(KG):
                nc.tensor.matmul_mx(
                    out=u[n, t][:],
                    lhsT=v_codes[j][:, kg, t].rearrange("p m b -> p (m b)").bitcast(FP4X4),
                    lhsT_scale=v_planes[j][:, kg, t],
                    rhs=a_codes[:, kg, 2 * CH * c : 2 * CH * (c + 1)].bitcast(FP4X4),
                    rhs_scale=a_planes[:, kg, CH * c : CH * (c + 1)],
                    start=(kg == 0),
                    stop=(kg == KG - 1),
                )

        def square(n, t):
            squares[n, t] = work.tile([P, CH], F32, tag="squares", name=f"squares{n}_{t}")
            nc.scalar.activation(squares[n, t][:], u[n, t][:], SQUARE)

        def cube(n, t):
            if t == 0:
                h_by_t[n] = work.tile(
                    [P, PACK, CH], BF16, tag="h_by_t", bufs=3, name=f"h_by_t{n}", align_bytes=64
                )
            nc.vector.scalar_tensor_tensor(
                out=h_by_t[n][:, t, :],
                in0=u[n, t][:],
                scalar=mob_cols[:, n % JG, t : t + 1],
                in1=squares[n, t][:],
                op0=MULT,
                op1=MULT,
            )

        def interleave(n, piece, engine):
            if n not in h_packed:
                h_packed[n] = work.tile(
                    [P, CH, PACK], BF16, tag="h_packed", bufs=3, name=f"h_packed{n}", align_bytes=64
                )
            x = slice(P * piece, P * (piece + 1))
            dst = h_packed[n][:, x, :].rearrange("p (c i) t -> p c t i", i=4)
            src = h_by_t[n][:, :, x].rearrange("p t (c i) -> p c t i", i=4)
            if engine == "scalar":
                nc.scalar.copy(dst, src)
            else:
                nc.vector.tensor_copy(out=dst, in_=src)

        def quantise(n, lo=0, hi=CH):
            nc.vector.quantize_mx(
                out=h_codes[n][:, lo:hi].bitcast(FP8X4),
                scales=h_planes[n][:, lo:hi],
                in_=h_packed[n][:, lo:hi, :].rearrange("p n t -> p (n t)"),
            )

        def place(c, pair, b):
            i, half = divmod(b, 2)
            return (CH // P) * c + 2 * pair + i, slice(NL * half, NL * (half + 1))

        def analyse(c, pair, b, j):
            row, cols = place(c, pair, b)
            n = JG * c + j
            x = slice(P * row - CH * c, P * (row + 1) - CH * c)
            if j == 0:
                z[c, pair, b] = psum.tile([P, NL], F32, tag=f"z{b}", bufs=1, name=f"z{c}_{pair}_{b}")
            nc.tensor.matmul_mx(
                out=z[c, pair, b][:],
                lhsT=h_codes[n][:, x].bitcast(FP8X4),
                lhsT_scale=h_planes[n][:, x],
                rhs=c_codes[:, j, cols].bitcast(FP8X4),
                rhs_scale=c_planes[4 * j : P, cols],
                start=(j == 0),
                stop=(j == JG - 1),
            )

        def subtract(c, pair, b):
            row, cols = place(c, pair, b)
            res[c, pair, b] = work.tile([P, NL], F32, tag="res", bufs=8, name=f"res{c}_{pair}_{b}")
            nc.vector.tensor_tensor(
                out=res[c, pair, b][:], in0=lin_rows[:, row, cols], in1=z[c, pair, b][:], op=SUBTRACT
            )

        def damp_and_store(c, pair, b, engine):
            row, cols = place(c, pair, b)
            r = res[c, pair, b]
            engine.tensor_tensor(out=r[:], in0=r[:], in1=damp_rows[:, cols], op=MULT)
            nc.sync.dma_start(out=out[P * row : P * (row + 1), cols], in_=r[:])

        def finish(c, pair, b):
            subtract(c, pair, b)
            damp_and_store(c, pair, b, nc.gpsimd)

        def analyse_all_groups(c, pair, b):
            for j in range(JG):
                analyse(c, pair, b, j)

        def second_product(n, t):
            if 2 <= n <= 4 and t >= 2:
                for b in (2 * t - 4, 2 * t - 3):
                    analyse(0, 0, b, n - 2)
            if n == 5 and t == 1:
                for b in range(BANKS):
                    analyse(0, 0, b, JG - 1)
            if n == 5 and t >= 2:
                finish(0, 0, t - 2)
                analyse_all_groups(0, 1, t - 2)
            if n == 6 and t == 0:
                analyse_all_groups(0, 1, 2)
            if n == 6 and t == 1:
                finish(0, 0, 3)
                analyse_all_groups(0, 1, 3)
            if n == 6 and t >= 2:
                finish(0, 1, t - 2)
                analyse(1, 0, t - 2, 0)
            if n == 7 and t < 2:
                finish(0, 1, t + 2)
                analyse(1, 0, t + 2, 0)

        permute_v(0)
        for t in range(PACK):
            field(0, t)
        square(0, 0)
        permute_v(1)
        for n in range(STEPS):
            for t in range(PACK):
                if n == 6 and t == 0:
                    finish(0, 0, 2)
                cube(n, t)
                if n < LAST:
                    field(n + 1, t)
                if t + 1 < PACK:
                    square(n, t + 1)
                elif n < LAST:
                    square(n + 1, 0)
                if n >= 1:
                    mover = "vector" if 2 <= n <= 4 and 1 <= t <= 2 else "scalar"
                    interleave(n - 1, t, mover)
                if t == 1 and 2 <= n < LAST:
                    quantise(n - 2)
                second_product(n, t)
            if n + 2 < JG:
                permute_v(n + 2)

        quantise(LAST - 2)
        for b in range(BANKS):
            analyse(1, 0, b, 1)
        for piece in range(PIECES):
            interleave(LAST, piece, "vector" if piece == 1 else "scalar")
        quantise(LAST, 0, CH // 2)
        quantise(LAST - 1)
        quantise(LAST, CH // 2, CH)
        for b in range(BANKS):
            analyse(1, 0, b, 2)
            analyse(1, 0, b, 3)
        for b in range(BANKS):
            finish(1, 0, b)
        for b in range(BANKS):
            analyse_all_groups(1, 1, b)
        subtract(1, 1, 0)
        for b in range(1, BANKS):
            subtract(1, 1, b)
            damp_and_store(1, 1, b - 1, nc.vector)
        damp_and_store(1, 1, BANKS - 1, nc.vector)
